import numpy as np, ml_dtypes
CORES = [2,6,10,14,18,22,26,30]
N = 8
BF = ml_dtypes.bfloat16
def gentries(a):
    return np.ascontiguousarray(a.reshape(8, 16, -1).transpose(0, 2, 1)).reshape(8, -1)
def gtable(e):
    e = np.asarray(e); return np.ascontiguousarray(e.reshape(8, -1, 16).transpose(0, 2, 1)).reshape(128, -1).astype(np.int32)
B, L, S, RO, ST = 3712, 128, 48, 3, 2
W = B + RO * S
def nodes(rng):
    v = 15 * rng.random((N, 8, 1, B)) + 8 * rng.random((N, 8, 1, B)) * rng.standard_normal((N, 8, 16, B), dtype=np.float32)
    return np.clip(np.rint(v), 0, 15).astype(np.int64)
def kids(rng, share):
    k = rng.integers(1, B, (N, 8, 16, B)); p = (rng.random((N, 8, 1, B)) < share) * rng.random((N, 8, 1, B))
    return np.where(rng.random(k.shape) < p, 0, k)
def ways(rng):
    j = rng.integers(1, B, (N, 8, RO, L - S)); pool = rng.integers(1, B, (N, 8, 48))
    e = np.take_along_axis(pool, rng.integers(0, 48, (N, 8, RO * L)), 2).reshape(N, 8, RO, L)
    return j, np.where(rng.random(e.shape) < 0.4, e, rng.integers(1, B, e.shape))
def far(rng, x, k, j, e):
    for q in range(N):
        for g in range(8):
            o = 1 + rng.permutation(B - 1)[:72]; a, w, v, z = o[:4], o[4:8], o[8:12], o[12:].reshape(4, 15)
            X, K = x[q, g], k[q, g]
            X[:, o] = 0; X[:, w] = 15; X[:, v] = 7; X[:, v[3]] = 15; X[rng.integers(0, 16), v[3]] = 14
            for i in (1, 2): X[:rng.integers(1, 16), z[i, 14]] = 1
            K[:, a[0]] = np.append(w[0], z[0])
            K[:, a[1]] = np.append(z[1], w[1])
            K[:, a[2]] = np.append(z[2], z[2, 0])
            K[:, a[3]] = np.concatenate([v[3:], z[3, :7], w[3:], z[3, 7:14]])
            j[q, g, 0, :4] = np.array([v[0], v[1], w[2], v[3]]); e[q, g, 0, :4] = a
            if rng.random() < 0.5: X[:, o] = 15 - X[:, o]
def pack(x, k, j, e):
    x = np.array(x); k = np.array(k); x[..., 0] = 0; k[..., 0] = 0
    return {"x": np.ascontiguousarray(x.reshape(N, 128, B)).astype(np.float32).astype(BF), "ch": np.ascontiguousarray(k.reshape(N, 128, B)).astype(np.int32),
            "jo": np.stack([gtable(a.reshape(8, -1)) for a in j]), "en": np.stack([gtable(a.reshape(8, -1)) for a in e])}
def setup_inputs(rng):
    share = rng.choice(np.array([0.05, 0.2, 0.4, 0.6]), (N, 8, 1, 1)); j, e = ways(rng)
    return pack(nodes(rng), kids(rng, share), j, e)
def setup_inputs_room(rng):
    x = nodes(rng); k = kids(rng, 0.3); j, e = ways(rng); h = (B - 1) // 2; m = L - S
    for q in range(N):
        for g in range(8):
            o = 1 + rng.permutation(B - 1); full, bare = o[:h], o[h:]
            k[q, g][:, full] = rng.choice(full, (16, h)); k[q, g][:, bare] = 0
            n = int(rng.choice(np.array([0, 1, S - 1, S, S + 1, m])))
            if q == 0: n = (S, S + 1, m, S - 1, 1, 0, S, S + 1)[g]
            stuck = rng.permutation(m) < n
            j[q, g, 0] = np.where(stuck, rng.choice(full, m), rng.choice(bare, m))
            e[q, g, 0, :m] = np.where(stuck, rng.choice(full, m), rng.permutation(bare)[:m])
    return pack(x, k, j, e)
def setup_inputs_ties(rng):
    a = rng.integers(0, 15, (N, 8, 16, 1)); x = a + rng.integers(0, 2, (N, 8, 16, B))
    x[:, 0:4:2] = a[:, 0:4:2] + rng.integers(0, 2, (N, 2, 1, B)); x[:, 3] = a[:, 3]; x[:, 4:] = nodes(rng)[:, 4:]
    j, e = ways(rng); k = kids(rng, 0.1)
    k[:, 1] = rng.integers(1, B, (N, 16, B)); k[:, 4:] = rng.integers(1, B, (N, 4, 16, B)); k[:, 4::2] = 0
    e[:, 4::2] = 1 + np.argsort(rng.random((N, 2, RO, B - 1)), axis=-1)[..., :L]
    for g, i in ((5, 15), (7, 0)):
        k[:, g, i] = k[:, g, i] * rng.integers(0, 2, (N, B))
    return pack(x, k, j, e)
def setup_inputs_alike(rng):
    share = np.full((N, 8, 1, 1), 0.15); share[:, 1] = 0.0; k = kids(rng, share); j, e = ways(rng)
    pool = rng.integers(1, B, (N, 4, 24)); pool[..., 0] = 1; pool[..., 1] = B - 1
    k[:, ::2] = np.where(k[:, ::2] > 0, np.take_along_axis(pool, rng.integers(0, 24, (N, 4, 16 * B)), 2).reshape(N, 4, 16, B), 0)
    k[:, 4, 0] = np.arange(B)
    e[:, 1] = rng.integers(1, B, (N, 1, 1)); j[:, 2] = e[:, 2, :, :L - S]
    e[:, 5] = rng.choice(np.array([1, B - 1]), (N, RO, L)); j[:, 5] = rng.choice(np.array([1, B - 1]), (N, RO, L - S))
    return pack(nodes(rng), k, j, e)
def setup_inputs_guests(rng):
    x = nodes(rng); k = np.zeros((N, 8, 16, B), np.int64); j, e = ways(rng); h = (B - 1) // 4; m = L - S; p = S // 2; at = np.arange(p + 1)
    for q in range(N):
        for g in range(8):
            o = 1 + rng.permutation(B - 1); kin = [o[i:h:4] for i in range(4)]; low, bare = o[h:2 * h], o[2 * h:]
            r, hub, rest = low[:p + 1], low[p + 1:2 * p + 2], low[2 * p + 2:]
            w = rng.integers(0, 4, m); w[0:S:2] = 0; w[1:S:2] = (np.arange(p) + q + g) % 4
            for i in range(4):
                x[q, g][:, kin[i]] = (8, 10, 12, 6)[i]; k[q, g][:, kin[i]] = rng.choice(kin[i], (16, kin[i].size))
                j[q, g, 0] = np.where(w == i, rng.choice(kin[i], m), j[q, g, 0])
                e[q, g, 0, :m] = np.where(w == i, rng.choice(kin[i], m), e[q, g, 0, :m])
            duel = (at < p - 1) & (at % 8 < 4) & (g % 2 == 0)
            via = duel | (at >= p - 1)
            u = rng.integers(0, 16, h); u[:p + 1][duel] = 0
            x[q, g][:, low] = 0; k[q, g][:, low] = rng.choice(rest, (16, h)); k[q, g][u, low] = 0
            k[q, g][:, hub] = r
            for t in range(1, RO):
                e[q, g, t] = rng.permutation(bare)[:L]
                if g == 7: continue
                if t == 1:
                    e[q, g, t, m:] = np.append(np.repeat(r[:p - 1], 2), r[p - 1:])
                    b = hub[via]; e[q, g, t, :b.size] = b; j[q, g, t, :b.size] = rng.choice(kin[2], b.size)
                else:
                    e[q, g, t, :p + 1] = r; j[q, g, t, :p + 1] = rng.choice(kin[2], p + 1)
                    b = r[duel]; e[q, g, t, p + 1:p + 1 + b.size] = b; j[q, g, t, p + 1:p + 1 + b.size] = rng.choice(kin[3], b.size)
    return pack(x, k, j, e)
def setup_inputs_spread(rng):
    x = np.floor(np.exp2(rng.integers(0, 5, (N, 8, 1, B))) * rng.random((N, 8, 16, B))).astype(np.int64); u = rng.random((N, 8, 1, B))
    x = np.where(u < 0.06, 0, np.where(u > 0.94, 15, x)); j, e = ways(rng)
    k = kids(rng, rng.random((N, 8, 1, 1)) ** 2)
    far(rng, x, k, j, e)
    return pack(x, k, j, e)
def check_inputs(d):
    bad = []; v = np.asarray(d["x"]).astype(np.float32)
    if not (np.min(v) >= 0 and np.max(v) <= 15) or np.any(v != np.floor(v)): bad.append("x whole and from 0 to 15")
    if np.any(v[..., 0] != 0): bad.append("column 0 of x")
    if np.any(d["ch"][..., 0] != 0): bad.append("column 0 of ch")
    for k, lo in (("ch", 0), ("jo", 1), ("en", 1)):
        if np.min(d[k]) < lo or np.max(d[k]) > B - 1: bad.append("range of " + k)
    return bad
def cols(t, n):
    return np.take_along_axis(t, n[:, :, None, :], 3)
def slot(t, i):
    return np.take_along_axis(t, i[:, :, None, :], 2)[:, :, 0]
def reference(x, ch, jo, en):
    xs = np.zeros((N, 8, 16, W), np.int64); xs[..., :B] = x.astype(np.float32).astype(np.int64).reshape(N, 8, 16, B)
    cl = np.zeros((N, 8, 16, W), np.int64); cl[..., :B] = ch.astype(np.int64).reshape(N, 8, 16, B)
    jl = np.stack([gentries(a) for a in jo]).astype(np.int64).reshape(N, 8, RO, L - S)
    el = np.stack([gentries(a) for a in en]).astype(np.int64).reshape(N, 8, RO, L)
    lower = np.tril(np.ones((L, L), bool), -1); guest = np.zeros((N, 8, S), bool); ends = []
    for rnd in range(RO):
        gid = np.zeros(S, np.int64) if rnd == 0 else B + (rnd - 1) * S + np.arange(S)
        c = np.concatenate([jl[:, :, rnd], np.broadcast_to(gid, (N, 8, S))], axis=2)
        n = el[:, :, rnd].copy()
        there = np.concatenate([np.ones((N, 8, L - S), bool), guest], axis=2); live = there.copy()
        for step in range(ST):
            before = (n[:, :, :, None] == n[:, :, None, :]) & live[:, :, None, :] & lower
            act = live & ~np.any(before, axis=3)
            xn = cols(xs, n); xc = cols(xs, c); k = cols(cl, n)
            kx = np.take_along_axis(xs, k.reshape(N, 8, 1, 16 * L), 3).reshape(N, 8, 16, 16, L)
            e = np.where(k == 0, 256, np.add.reduce(np.abs(kx - xn[:, :, :, None, :]), axis=2))
            i = np.argmax(e, axis=2); top = slot(e, i)
            has = top == 256
            put = act & (top > np.add.reduce(np.abs(xc - xn), axis=2)); go = act & ~has
            o = np.where(put & ~has, slot(k, i), c)
            s = np.add.reduce(np.abs(kx - cols(xs, o)[:, :, :, None, :]), axis=2)
            s = np.where(put[:, :, None, :] & (np.arange(16)[:, None] == i[:, :, None, :]), 999, s)
            nxt = slot(k, np.argmin(s, axis=2))
            q, g, l = np.nonzero(put); w = n[q, g, l]
            cl[q, g, i[q, g, l], w] = c[q, g, l]
            xs[q, g, :, w] = ((xc + xn) >> 1)[q, g, :, l]
            c = np.where(go, o, c); n = np.where(go, nxt, n); live = live & ~(act & has)
        place = np.add.accumulate(live.astype(np.int64), axis=2) - 1
        q, g, l = np.nonzero(live & (place < S)); p = place[q, g, l]; to = (q + 1 + rnd) % N
        xs[to, g, :, B + rnd * S + p] = xs[q, g, :, c[q, g, l]]
        guest = np.zeros((N, 8, S), bool); guest[to, g, p] = True
        ends.append(np.where(there, n, 0))
    yl = cols(cl, np.concatenate(ends, axis=2))
    return {"yx": xs.reshape(N, 128, W).astype(np.float32).astype(BF), "yl": yl.reshape(N, 128, RO * L).astype(np.float32)}

import numpy as np
from concourse.mybir import AluOpType as ALU, ActivationFunctionType as ACT

B, L, S, RO = 3712, 128, 48, 3
WD = B + RO * S
TW = 4096
SC = 69632.0
BIG = float(2 ** 27)
BQ = 8192.0
NCH = 4

SCRATCH = {}
for _dt, _txt in (
    ("bfloat16", "xt:4096 ib:128 nib:128 hi2:2,128 qi:2,128 qx:2,128 bi2:2,128 nu:128 t4:4,128 b2s:8,16 bns:8,16 bbg:8,16 b8:4,8 "
                 "mskb:8,16 cof:128 cpl:128 selp:8,128 seln:8,128 ones:128 o64:128 kc1:8,32 kc2:8,32 qc:4,128 na1:24,32 m2:8,16 nbg:16 "
                 "ibk:8,32 ibn:8,32 livn:8,16 eq:8,128 kx0:2048 kx1:2048 m0:2048 m1:2048 xn:128 xc:128 xo0:128 xo1:128 mc:128 dl:128 xs:128 "
                 "sel0:8,16 sel1:8,16 bps:8,16 npt:8,16 dead0:8,32 dead1:8,32 live:8,16 qv:2,128 ab:128 "
                 "snd0:256 snd1:256 snd2:256 lnd0:48 lnd1:48 lnd2:48"),
    ("float32", "chf:4096 tab:4096 cr2:128 j1:128 jd:8,16 jm:8,16 pf:8 i32:128 bex:8,16 a32:8 a16:3,8 msk:8,16 rst:32 vm:128 vm2:128 "
                "top1:8,32 top2:256 top3:8,32 top4:256 top5:8,32 tm3:8,16 zer:256 tm1:8,16 tm2:8,16 qk:2,128 pres:384 ylt:384"),
    ("int32", "chi:3712 eni:24 joi:16 cwi:24 pin:4 wi:8 wj:8 wi2:8 wj2:8 endi:24 endj:24"),
    ("uint16", "enu:24 cwu:24 of1:24 of2:8 plu:8 ku:128 ou:8 nu2:8 endu:24"),
    ("float16", "nr1:384 cr1:384 nr2:128 kf0:128 kf1:128"),
):
    for _w in _txt.split():
        SCRATCH[_w.split(":")[0]] = ("sbuf", [128] + [int(_k) for _k in _w.split(":")[1].split(",")], _dt)
for _k, _sh in enumerate(([512], [512], [512], [16, 32], [512], [512], [512], [4, 128])):
    SCRATCH["p%d" % _k] = ("psum", [128] + _sh, "float32")
SEMAPHORES = ["cv", "cs", "cp", "cg", "den", "djo", "dx", "dox", "dol", "dol2", "dog", "sent", "ar0", "ar1", "ar2"] + ["dc%d" % k for k in range(NCH)]

SPLIT = {(0, 0): (20, 20), (0, 1): (8, 14), (1, 0): (30, 30), (1, 1): (16, 24), (2, 0): (30, 30), (2, 1): (14, 24)}
CY, PE, GA, SCA, LAT, FIX, RATE, DMA0, REM = np.array([
    [1.0, 0.5, 1.56, 3.8, 70.0, 15.0, 260.0, 1800.0, 2500.0], [1.0, 0.45, 1.56, 3.8, 110.0, 30.0, 400.0, 1500.0, 2000.0],
    [0.9, 0.42, 1.2, 2.5, 40.0, 5.0, 200.0, 2000.0, 2500.0], [1.2, 0.55, 1.9, 5.0, 90.0, 15.0, 300.0, 1800.0, 3500.0]]).T
TRIES, SEED, SHAKE, SPAN = 700, 4, 700.0, 1500.0
ALL = slice(None)
R_ = slice
ORDER = []


def schedule(ops):
    n = len(ops)
    eng = [o["e"] for o in ops]
    one = np.ones(len(CY))
    costs = [o["cost"] * one for o in ops]
    tails = [o["extra"] * one for o in ops]
    preds = [[(d, costs[d] + (0.0 if k == 0 else LAT + tails[d] if k == 1 else REM * k)) for d, k in o["deps"].items()] for o in ops]
    cost = [float(c[0]) for c in costs]
    tail = [float(c[0]) for c in tails]
    pred = [[(d, float(v[0]) - cost[d]) for d, v in p] for p in preds]
    succ = [[] for _ in ops]
    for i in range(n):
        for d, gap in pred[i]:
            succ[d].append((i, gap))
    zero = [0.0] * n

    def replay(at):
        free = {e: 0.0 * one for e in set(eng)}
        t = [None] * n
        end = 0.0 * one
        for i in sorted(range(n), key=lambda i: (at[i], i)):
            t0 = free[eng[i]]
            for d, v in preds[i]:
                t0 = np.maximum(t0, t[d] + v)
            t[i] = t0
            free[eng[i]] = t0 + costs[i]
            if tail[i]:
                end = np.maximum(end, free[eng[i]] + tails[i])
        return end

    def place(order, before, lead):
        busy = {e: [] for e in set(eng)}
        at = [0.0] * n
        for i in order:
            t0 = lead[i]
            for d, gap in before[i]:
                t0 = max(t0, at[d] + cost[d] + gap)
            row = busy[eng[i]]
            j = len(row)
            while j and row[j - 1][0] >= t0 + cost[i]:
                j -= 1
            while True:
                if j:
                    t0 = max(t0, row[j - 1][1])
                if j == len(row) or t0 + cost[i] <= row[j][0]:
                    break
                j += 1
            row.insert(j, (t0, t0 + cost[i]))
            at[i] = t0
        return at

    def both(at):
        back = place(sorted(range(n), key=lambda i: (-at[i] - cost[i], -i)), succ, tail)
        at = place(sorted(range(n), key=lambda i: (-back[i] - cost[i], i)), pred, zero)
        return (max(at[i] + cost[i] + tail[i] for i in range(n)), at)

    level = [0.0] * n
    for i in range(n - 1, -1, -1):
        level[i] = cost[i] + max([tail[i]] + [level[d] + gap for d, gap in succ[i]])
    best = both(both(place(sorted(range(n), key=lambda i: (-level[i], i)), pred, zero))[1])
    rng = np.random.default_rng(SEED)
    base = replay(best[1])
    score = float(len(CY))
    for k in range(TRIES):
        mid = rng.random() * best[0]
        shake = rng.normal(0.0, SHAKE, n)
        key = [t + (shake[i] if abs(t - mid) < SPAN else 0.0) for i, t in enumerate(best[1])]
        for i in range(n):
            for d, gap in pred[i]:
                key[i] = max(key[i], key[d] + 0.01)
        new = both(place(sorted(range(n), key=lambda i: (key[i], i)), pred, zero))
        if new[0] <= best[0] + 400.0:
            mark = float(np.sum(replay(new[1]) / base))
            if mark <= score:
                best, score = new, mark
    return best[1]


def rank_program(g, core, T, topo):
    rank = T.rank_of(core)
    if rank is None:
        return
    N = len(T.cores)
    Q = {"v": g.vector, "s": g.scalar, "p": g.tensor, "g": g, "y": g.sync}
    CNT = {"v": "cv", "s": "cs", "p": "cp", "g": "cg"}
    ops, hist, bank, masks = [], {}, {}, {}

    def A(name, *idx):
        key = (name, str(idx[1:]))
        if key not in masks:
            m = np.zeros(SCRATCH[name][1][1:], bool)
            m[idx[1:]] = True
            masks[key] = (int.from_bytes(np.packbits(m.reshape(-1)).tobytes(), "big"), int(m.sum()))
        return (T[name][idx], [(name, masks[key][0])], [], masks[key][1], 4 if "32" in SCRATCH[name][2] else 2, SCRATCH[name][0])

    def H(ap):
        return (ap, [], [], 0, 0, "hbm")

    def IND(win, off):
        return (win[0].indirect(off[0]), win[1], off[1], 16 * off[3], win[4], "ind")

    def rec(e, fn, outs, ins, cost, extra=0.0, sem=None, inc=1, tok=None, after=(), grp=None):
        me = len(ops)
        acc = [(b, m, True) for a in outs for b, m in a[1]] + [(b, m, False) for a in ins for b, m in a[1]]
        acc += [(b, m, False) for a in outs + ins for b, m in a[2]]
        deps = {d: 0 for d in after}
        for b, m, w in acc:
            if SCRATCH[b][0] == "psum":
                st = bank.setdefault(b, {"e": e, "cur": [], "prev": [], "start": None})
                if st["e"] != e:
                    st["e"], st["prev"], st["cur"] = e, st["cur"], []
                for d in st["prev"]:
                    deps[d] = 1
                if e == "p":
                    if grp[0] or grp[1]:
                        for d in st["cur"]:
                            deps.setdefault(d, 0)
                    if grp[0]:
                        st["start"] = me
                    else:
                        deps.setdefault(st["start"], 0)
                st["cur"].append(me)
            if SCRATCH[b][0] != "psum" or e != "p":
                h = hist.setdefault(b, [])
                for d, m2, w2 in h:
                    if (w or w2) and (m & m2) and d != me:
                        deps[d] = 1
                if w:
                    h[:] = [x for x in h if x[1] & ~m]
                h.append((me, m, w))
        deps.pop(me, None)
        if tok:
            deps[tok[1]] = tok[2]
        ops.append({"e": e, "fn": fn, "cost": cost, "extra": extra, "sem": sem or CNT[e], "inc": inc, "tok": tok and tok[0], "deps": deps})
        return me

    def sv(x):
        return x[0] if isinstance(x, tuple) else x

    def aps(*xs):
        return [x for x in xs if isinstance(x, tuple)]

    def cost(out, a, per):
        if out[5] == "ind":
            return 50 + out[3] * SCA * CY
        if a[5] == "ind":
            return 55 + out[3] * GA * CY
        return FIX + max(64, out[3] * per) * CY

    def half(out, a):
        return 0.5 if out[4] == 2 and a[4] == 2 else 1

    def mm(out, lhsT, rhs, start=False, stop=False, after=()):
        return rec("p", lambda: g.tensor.matmul(out[0], lhsT[0], rhs[0], start, stop), [out], [lhsT, rhs],
                   max(min(64, lhsT[3]), rhs[3]) * PE * (4 if rhs[4] == 4 else 1), grp=(start, stop), after=after)

    def cp(out, a):
        return rec("v", lambda: g.vector.tensor_copy(out[0], a[0]), [out], [a], cost(out, a, half(out, a)))

    def tt(out, a, b, op):
        return rec("v", lambda: g.vector.tensor_tensor(out[0], a[0], b[0], op), [out], [a, b], cost(out, a, 1 if "psum" in (a[5], b[5]) else 2))

    def ts(out, a, s1, op0, s2=None, op1=None):
        c = cost(out, a, half(out, a))
        if op1 is None:
            return rec("v", lambda: g.vector.tensor_scalar(out[0], a[0], sv(s1), None, op0), [out], aps(a, s1), c)
        return rec("v", lambda: g.vector.tensor_scalar(out[0], a[0], sv(s1), sv(s2), op0, op1), [out], aps(a, s1, s2), c)

    def ms(out, c):
        return rec("v", lambda: g.vector.memset(out[0], c), [out], [], cost(out, out, half(out, out)))

    def scan(o, d0, d1):
        rec("v", lambda: g.vector.tensor_tensor_scan(o[0], d0[0], d1[0], -1e9, ALU.add, ALU.max), [o], [d0, d1], cost(o, o, 1))

    def act(out, a, f=None, bias=0.0, scale=1.0, tok=None, more=0.0):
        f = f or ACT.Identity
        return rec("s", lambda: g.scalar.activation(out[0], a[0], f, bias=sv(bias), scale=sv(scale)), [out], aps(a, bias, scale),
                   cost(out, a, 1) + more, tok=tok)

    def iota(out, pat, base, cm, flt=True):
        c = 130 + 2 * out[3] * CY
        if flt:
            return rec("g", lambda: g.iota(out[0], pat, base, cm, allow_small_or_imprecise_dtypes=True), [out], [], c)
        return rec("g", lambda: g.iota(out[0], pat, base, cm), [out], [], c)

    def fill(out, c):
        return iota(out, [[0, out[3]]], c, 0, out[1][0][0] != "endi")

    queued = [0.0]

    def dma(q, out, a, sem, load=False, after=(), tok=None):
        sb = out if load else a
        t = sb[3] * sb[4] * 128 / RATE
        if load:
            queued[0] = queued[0] + t
            t = queued[0]
        return rec(q, lambda: Q[q].dma_start(out[0], a[0]), [out], [a], 60.0, DMA0 + t, sem, 16, after=after, tok=tok)

    X = A("xt", ALL, R_(0, TW))
    CH = A("chf", ALL, R_(0, TW))
    TAB = A("tab", ALL, R_(0, TW))
    W2 = lambda name: A(name, ALL, ALL)
    W3 = lambda name: A(name, ALL, ALL, ALL)
    col = lambda name, j: A(name, ALL, R_(j, j + 1))
    row = lambda name, j: A(name, ALL, j, ALL)
    lr = lambda name, nl: A(name, R_(0, nl), ALL, ALL)
    lo = lambda name, nl: A(name, R_(0, nl), ALL, R_(0, 16))
    rr = lambda name, nl, lo=0: A(name, ALL, R_(lo, lo + nl))
    pr = lambda name, nl, lo, w: A(name, R_(0, nl), R_(lo, lo + w))
    w8 = lambda name, nl, lo=0: A(name, ALL, R_(lo, lo + nl // 16))
    key = lambda b, nl, lo, hi: A(b, R_(0, nl), R_(0, 8), R_(lo, hi))
    toplr = lambda top, nl: A(top, R_(0, nl), ALL, R_(16, 32))
    livn = lambda nl, gi: A("livn", R_(0, nl), gi, ALL)
    lanes = lambda t: L - S if t == 0 else L
    na1 = lambda t, w=16: A("na1", R_(0, lanes(t)), R_(8 * t, 8 * t + 8), R_(0, w))
    a32 = lambda nl: pr("a32", nl, 0, nl // 16)

    def eye(name, nl, j=None):
        return A(name, R_(0, nl), R_(0, nl)) if j is None else A(name, R_(0, nl), j, R_(0, nl))

    dma("s", W2("eni"), H(T.en[:]), "den", True)
    dma("s", A("joi", ALL, R_(0, 15)), H(T.jo[:]), "djo", True)
    cw = B // NCH
    prev = []
    for k in range(NCH):
        prev = [dma("y", rr("chi", cw, k * cw), H(T.ch[:, k * cw:(k + 1) * cw]), "dc%d" % k, True, prev)]
        cp(rr("chf", cw, k * cw), rr("chi", cw, k * cw))
    mark = ms(col("xt", 0), 48.0)
    ops[dma("y", rr("xt", B - 1, 1), H(T.x[:, 1:B]), "dx", True, prev)]["deps"][mark] = 1

    J1, I32, BEX, MSK, IB, NIB = W2("j1"), W2("i32"), W3("bex"), W3("msk"), W2("ib"), W2("nib")
    iota(rr("tab", 512), [[1, 512]], -2048, 0)
    act(rr("tab", 512, 512), rr("tab", 512), bias=512.0)
    act(rr("tab", 1024, 1024), rr("tab", 1024), bias=1024.0)
    act(rr("tab", 1024, 2048), rr("tab", 1024), bias=2048.0)
    iota(col("pin", 0), [[0, 1]], 0, 1, False)
    iota(J1, [[1, 128]], 0, -1)
    iota(W3("jd"), [[1, 8], [0, 16]], 0, 0)
    iota(W3("jm"), [[0, 8], [1, 16]], 0, 0)
    iota(W2("cwi"), [[S, 3], [16, 8]], B - S - 80, 0, False)
    iota(rr("tab", 1024, 3072), [[1, 1024]], 1024, 0)
    for k in ("kc1", "kc2"):
        iota(A(k, R_(0, 64), ALL, ALL), [[0, 8], [-4096, 32]], 14 * 4096 + 2048, 0)
        ms(A(k, R_(64, 128), ALL, ALL), 0.0)
    ms(A("kc1", R_(0, 64), ALL, R_(16, 32)), 15 * 4096.0 + 2048.0)
    ms(A("kc2", R_(0, 64), ALL, R_(16, 32)), -float(2 ** 24))
    ms(A("kc2", R_(64, 128), ALL, R_(16, 32)), 4096.0 + 2048.0)
    ms(W2("ones"), 1.0)
    fill(rr("xt", TW - B, B), 0)
    fill(rr("chf", TW - B, B), 0)
    ts(col("pin", 1), col("pin", 0), 4, ALU.arith_shift_right)
    ts(col("pin", 2), col("pin", 0), 15, ALU.bitwise_and)
    cp(rr("pf", 3), rr("pin", 3))
    ts(I32, J1, 0.0, ALU.is_equal)
    ts(BEX, W3("jd"), col("pf", 1), ALU.is_equal)
    ts(MSK, W3("jm"), col("pf", 2), ALU.is_equal)
    act(col("pf", 3), col("pf", 0), bias=-float(WD), scale=-1.0)
    act(col("pf", 4), col("pf", 0), bias=128.0)
    act(col("pf", 5), col("pf", 0), bias=float(2 ** 22))
    cp(W2("enu"), W2("eni"))
    ts(W2("cwi"), W2("cwi"), col("pf", 2), ALU.add)
    for t in range(RO):
        cp(rr("cwi", 5, 8 * t), rr("joi", 5, 5 * t))
    cp(W2("cwu"), W2("cwi"))
    act(W2("a32"), A("bex", ALL, ALL, 0))
    for j, c in enumerate((1.0 / 16, -1.0 / 16, -1.0)):
        act(row("a16", j), A("bex", ALL, ALL, 0), scale=c)
    for gi in range(8):
        act(row("selp", gi), W2("ones"), scale=A("a16", ALL, 0, R_(gi, gi + 1)))
        ts(row("seln", gi), W2("ones"), A("a16", ALL, 1, R_(gi, gi + 1)), ALU.mult)
    ts(row("t4", 0), J1, 0.0, ALU.is_le, 0.5, ALU.mult)
    cp(row("t4", 1), row("t4", 0))
    cp(A("t4", ALL, R_(2, 4), ALL), A("t4", ALL, R_(0, 2), ALL))
    ts(W2("cof"), MSK, -float(2 ** 40), ALU.mult, float(2 ** 40), ALU.add)
    act(W3("m2"), MSK, scale=-2048.0)
    ms(W2("nbg"), -BIG)
    ts(W2("cpl"), MSK, col("pf", 5), ALU.mult, -float(2 ** 22), ALU.add)
    ts(W2("nu"), J1, 0.0, ALU.is_gt, -1.0, ALU.mult)
    for t in range(RO):
        cp(rr("nr1", lanes(t), 128 * t), IND(TAB, w8("enu", lanes(t), 8 * t)))
        cp(rr("cr1", lanes(t), 128 * t), IND(TAB, w8("cwu", lanes(t), 8 * t)))
    for out, c in ((IB, 1.0), (NIB, -1.0), (row("qi", 0), -BQ), (row("qi", 1), BQ), (row("hi2", 0), 0.5), (row("hi2", 1), -0.5),
                   (row("bi2", 0), -BIG), (row("bi2", 1), BIG), (row("qx", 0), -64.0), (row("qx", 1), 64.0)):
        act(out, I32, scale=c)
    for out, c in ((W3("b2s"), 2 * SC), (W3("bns"), -SC), (W3("bps"), SC), (W3("bbg"), BIG / 16)):
        act(out, BEX, scale=c)
    for j, c in enumerate((-SC, 2 * SC, SC, -2 * SC)):
        act(row("b8", j), W2("a32"), scale=c)
    act(W3("mskb"), MSK, ACT.Sigmoid, bias=-200.0, scale=400.0, more=1300.0)
    mm(A("p3", ALL, R_(8, 16), R_(0, 16)), IB, W3("mskb"), True, True)
    mm(rr("p4", 128, 256), IB, W3("mskb"), True, True)
    for k in ("na1", "dead0", "dead1", "ibk", "ibn"):
        fill(W3(k), 0)
    fill(W2("zer"), 0)
    ms(A("zer", ALL, R_(0, 256, 32)), -1e9)
    act(A("ibk", ALL, ALL, R_(0, 16)), I32)
    act(A("ibn", ALL, ALL, R_(16, 32)), I32)
    ms(W2("o64"), 1.0 / 64)
    for j, c in enumerate((2048.0, 2048.0 - BQ, -192.0, -64.0)):
        ms(row("qc", j), c)
    ms(W2("rst"), 0.0)
    fill(W2("ab"), 0)
    fill(W2("pres"), 1)
    fill(rr("pres", S, 80), 0)
    fill(W2("endi"), 0)
    for t in range(RO):
        fill(W2("snd%d" % t), 0)

    def pairs(nl, nr, live, na, dead, off):
        for h in range(2):
            b = "p%d" % (5 + h)
            mm(pr(b, nl, 0, 4 * nl), nr, A("seln", ALL, R_(4 * h, 4 * h + 4), R_(0, nl)), True)
            for j in range(4):
                mm(pr(b, nl, j * nl, nl), A("selp", ALL, 4 * h + j, R_(0, nl)), nr, False, j == 3)
            tt(A("eq", R_(0, nl), R_(4 * h, 4 * h + 4), R_(0, nl)), pr(b, nl, 0, 4 * nl), A("t4", R_(0, nl), ALL, R_(0, nl)), ALU.is_equal)
        if na:
            for gi in range(8):
                mm(pr("p5", nl, 16 * gi, 16), eye("eq", nl, gi), live(gi), True, True)
            act(na, pr("p5", nl, 0, 128))
        v = pr("p6", nl, 0, 128)
        mm(v, eye("ib", nl), A("cof", R_(0, nl), ALL), True)
        mm(v, nr, NIB)
        mm(v, eye("ib", nl), lr("m2", nl))
        if dead is not None:
            mm(v, eye("bi2", nl, 0), dead)
        for gi in range(8):
            mm(pr("p6", nl, 16 * gi, 16), eye("eq", nl, gi), live(gi), False, gi == 7)
        offsets(nl, 3, off, "vm", ALU.max, ALU.min, A("a16", R_(0, nl), 2, R_(0, nl // 16)))

    def offsets(nl, j, off, vm, op0, op1, a):
        ts(pr(vm, nl, 0, 128), pr("p6", nl, 0, 128), pr("pf", nl, j, 1), op0, 0.0, op1)
        mm(w8("p5", nl, 128), pr(vm, nl, 0, 128), a, True, True)
        cp(off, w8("p5", nl, 128))

    def pre_act(t):
        nl = lanes(t)
        pairs(nl, rr("nr1", nl, 128 * t), lambda gi: A("nbg", R_(0, nl), ALL), na1(t), None, w8("of1", nl, 8 * t))

    def engines_of(src):
        ds = [T.cores[(T.rank_of(src) + 1 + t) % N] for t in range(RO)]
        return [e for e in topo.engines(src, ds[0]) if all(e in topo.engines(src, d) for d in ds)]

    mine = engines_of(core)
    sent = {}

    def pack_send(t):
        nl = lanes(t)
        act(rr("xs", nl), IND(X, w8("ou", nl)), bias=16.0 if t < RO - 1 else 0.0)
        cp(IND(A("snd%d" % t, ALL, R_(0, 256)), w8("plu", nl)), rr("xs", nl))
        rid, pid, _ = topo.addr(T.cores[(rank + 1 + t) % N])
        src = rr("snd%d" % t, S)

        def fn():
            g.remote_dma(T["lnd%d" % t][:, :], src[0], T.sem["ar%d" % t], T.sem["sent"], pid, rid, sum(1 << e for e in mine))
        sent[t] = rec("g", fn, [], [src], 100.0, 500.0, "sent", len(mine))

    def arrived(t):
        return (("ar%d" % t, len(engines_of(T.cores[(rank - 1 - t) % N]))), sent[t], 1.8 if t == 0 else 1.01)

    def gather_kx(kx, lo, hi, e, sign):
        if hi <= lo:
            return
        out = A(kx, ALL, R_(16 * lo, 16 * hi))
        src = IND(X, A("ku", ALL, R_(lo, hi)))
        if e == "s":
            act(out, src, scale=sign)
        elif sign > 0:
            cp(out, src)
        else:
            ts(out, src, -1.0, ALU.mult)

    def slot(b, nl, src, s, j, **kw):
        out = A(b, R_(0, nl), R_(0, 8), s) if b == "p3" else A(b, R_(0, nl), R_(s, 256, 32))
        return mm(out, A(src, ALL, R_(s, 16 * nl, 16)), row("b8", j), **kw)

    def relu_part(d, kx, m, xv, l0, h, k, sign):
        part = R_(16 * l0 + k, 16 * (l0 + h), 2)
        mm(rr(d, 8 * h), IB, A(kx, ALL, part), True)
        for j in range(8):
            mm(A(d, ALL, R_(j, 8 * h, 8)), sign, rr(xv, h, l0), False, j == 7)
        act(A(m, ALL, part), rr(d, 8 * h), ACT.Relu)

    def distances(xv, kx, m, nl, b, j0, j1, aside=False):
        h = nl // 2
        shift = [mm(pr(b, h, 32 * gi, 16), rr(xv, h), row("bps", gi)) for gi in range(8)] if aside else []
        first = [slot(b, nl, kx, s, j0) for s in range(16)]
        if not aside:
            for j in range(8):
                mm(A("p0", ALL, R_(j, 8 * h, 8)), NIB, rr(xv, h), True, True)
        for k in range(2):
            if aside:
                relu_part("p6", kx, m, xv, 0, h, k, IB)
            else:
                tt(A(m, ALL, R_(k, 16 * h, 2)), A(kx, ALL, R_(k, 16 * h, 2)), rr("p0", 8 * h), ALU.max)
            relu_part("p6" if aside else "p%d" % (1 + k), kx, m, xv, h, h, k, NIB)
        for s in list(range(0, 16, 2)) + list(range(1, 16, 2)):
            slot(b, nl, m, s, j1, after=shift + [first[s]], stop=s == 15)

    def low_bits(tm, nl, wi, wj, out, b="p0"):
        mm(w8(b, nl), tm, a32(nl), True, True)
        cp(wi, w8(b, nl))
        if out:
            ts(wj, wi, 4095, ALU.bitwise_and)
            cp(out, wj)

    def second(t, st, nr):
        nl = lanes(t)
        aside = st == 1 and t < RO - 1
        b = "p5" if aside else "p4"
        k2 = pr(b, nl, 0, 256)
        mm(k2, rr("o64", nl), W3("kc2"), True)
        mm(k2, rr("kf%d" % st, nl), W3("ibk"))
        mm(k2, nr, W3("ibn"))
        mm(k2, eye("bi2", nl, 0), lr("dead%d" % st, nl))
        if st == 0:
            mm(k2, eye("ib", nl), na1(t, 32))
        for gi in range(8):
            kg = pr(b, nl, 32 * gi, 16)
            mm(kg, eye("bi2", nl, 0), A("sel%d" % st, R_(0, nl), gi, ALL))
            if st == 1:
                mm(kg, eye("eq", nl, gi), livn(nl, gi))
        distances("xo%d" % st, "kx%d" % st, "m%d" % st, nl, b, 2, 3, aside)
        flat, top, tm = ("top4", "top5", "tm3") if aside else ("top2", "top3", "tm2")
        scan(pr(flat, nl, 0, 256), pr("zer", nl, 0, 256), k2)
        act(lr(top, nl), pr(flat, nl, 0, 256))
        tt(lr(tm, nl), toplr(top, nl), lr("msk", nl) if aside else pr("p4", nl, 256, 128), ALU.mult)
        if st == 0:
            low_bits(lr(tm, nl), nl, w8("wi2", nl), w8("wj2", nl), w8("nu2", nl))
        else:
            low_bits(lr(tm, nl), nl, w8("endi", nl, 8 * t), None, None, "p6" if aside else "p0")

    def step(t, st):
        nl = lanes(t); h = nl // 2
        kx, m, kf, dead, sel = "kx%d" % st, "m%d" % st, "kf%d" % st, "dead%d" % st, "sel%d" % st
        vb, va = SPLIT[(t, st)]
        last = t == RO - 1 and st == 1
        guests = st == 0 and t > 0
        if st == 0:
            nw, nr, cr, off, icr = w8("enu", nl, 8 * t), rr("nr1", nl, 128 * t), rr("cr1", nl, 128 * t), w8("of1", nl, 8 * t), IB
            act(rr("xc", L - S), IND(X, rr("cwu", 5, 8 * t)))
        else:
            nw, nr, cr, off, icr = w8("nu2", nl), rr("nr2", nl), rr("cr2", nl), w8("of2", nl), I32
            cp(nr, IND(TAB, nw))
            pairs(nl, nr, lambda gi: livn(nl, gi), None, lo("dead0", nl), off)
        cp(rr("ku", nl), IND(CH, nw))
        act(rr("xn", nl), IND(X, nw))
        ts(rr(kf, nl), rr("ku", nl), -2048.0, ALU.add)
        gather_kx(kx, h + vb, nl, "s", 1.0)
        gather_kx(kx, h, h + vb, "v", 1.0)
        gather_kx(kx, va, h, "s", -1.0)
        gather_kx(kx, 0, va, "v", -1.0)
        if last:
            ms(col("xt", 0), 0.0)
        if guests:
            raw = W2("lnd%d" % (t - 1))
            act(rr("xc", S, 80), raw, ACT.Relu, bias=-16.0, tok=arrived(t - 1))
            act(rr("ab", S, 80), raw, ACT.Relu, bias=1.0, scale=-1.0, tok=arrived(t - 1))
            act(rr("xt", S, B + S * (t - 1)), rr("xc", S, 80))
            act(rr("pres", S, 128 * t + 80), rr("ab", S, 80), bias=1.0, scale=-1.0)
        e = A("p7", ALL, 0, R_(0, nl))
        mm(e, row("hi2", 1), rr("xn", nl), True)
        mm(e, row("hi2", 0), rr("xc", nl), False, True)
        act(rr("mc", nl), e, ACT.Relu, scale=2.0)
        act(rr("dl", nl), e, bias=191.75)
        mm(key("p3", nl, 0, 32), rr("o64", nl), W3("kc1"), True)
        mm(key("p3", nl, 16, 32), cr, icr)
        mm(key("p3", nl, 0, 16), rr(kf, nl), IB)
        if st == 0:
            mm(key("p3", nl, 0, 16), eye("ib", nl), na1(t))
        else:
            mm(key("p3", nl, 16, 32), eye("bi2", nl, 1), lo("dead0", nl))
            for gi in range(8):
                mm(A("p3", R_(0, nl), gi, R_(0, 16)), eye("eq", nl, gi), livn(nl, gi))
        if guests:
            mm(key("p3", nl, 16, 32), rr("ab", nl), W3("bbg"))
        a = mm(key("p3", nl, 16, 32), rr("xc", nl), W3("bns"))
        mm(key("p3", nl, 16, 32), rr("mc", nl), W3("b2s"), after=[a])
        distances("xn", kx, m, nl, "p3", 0, 1)
        q = lambda a, b2: A("p7", ALL, R_(a, b2), R_(0, nl))
        q1 = lambda a: A("p7", ALL, a, R_(0, nl))
        mm(q(0, 4), IB, A("qc", ALL, ALL, R_(0, nl)), True)
        for a, l_, r_ in ((2, IB, rr("xn", nl)), (3, IB, rr("xn", nl)), (2, IB, rr("dl", nl)), (1, icr, cr), (0, IB, rr(kf, nl))):
            mm(q1(a), l_, r_)
        for gi in range(8):
            scan(A("top1", R_(0, nl), gi, ALL), A("rst", R_(0, nl), ALL), A("p3", R_(0, nl), gi, ALL))
        top = toplr("top1", nl)
        tt(lr("tm1", nl), top, A("p3", R_(0, nl), R_(8, 16), R_(0, 16)), ALU.mult)
        tt(lr("npt", nl), top, key("p3", nl, 16, 32), ALU.is_equal)
        tt(lr(sel, nl), top, key("p3", nl, 0, 16), ALU.is_equal)
        act(lo(dead, nl), top, ACT.Sigmoid, bias=-18e6)
        low_bits(lr("tm1", nl), nl, w8("wi", nl), w8("wj", nl), w8("ou", nl))
        mm(q(2, 4), lr("npt", nl), A("qx", R_(0, nl), ALL, R_(0, nl)))
        mm(q(0, 2), lr(sel, nl), A("qi", R_(0, nl), ALL, R_(0, nl)), False, True)
        act(A("qk", ALL, ALL, R_(0, nl)), q(0, 2), ACT.Relu)
        act(A("qv", ALL, ALL, R_(0, nl)), q(2, 4), ACT.Relu)
        act(rr("xo%d" % st, nl), IND(X, w8("ou", nl)))
        tt(IND(CH, off), A("qk", ALL, 0, R_(0, nl)), A("qk", ALL, 1, R_(0, nl)), ALU.add)
        tt(IND(X, off), A("qv", ALL, 0, R_(0, nl)), A("qv", ALL, 1, R_(0, nl)), ALU.add)
        if st == 0:
            act(lr("live", nl), top, ACT.Sigmoid, bias=18e6, scale=-1.0)
            act(lr("livn", nl), lr("live", nl), scale=-BIG)
            act(rr("cr2", nl), IND(TAB, w8("ou", nl)))
            act(rr("xc", nl), IND(X, w8("ou", nl)))
        else:
            if last:
                dma("y", H(T.yx[:, 0:WD - S]), rr("xt", WD - S), "dox")
            v = pr("p6", nl, 0, 128)
            mm(v, eye("ib", nl), A("cpl", R_(0, nl), ALL), True)
            mm(v, eye("nu", nl), lo(dead, nl))
            mm(v, eye("qi", nl, 1), lo(dead, nl), False, True)
            offsets(nl, 4, w8("plu", nl), "vm2", ALU.min, ALU.max, a32(nl))
            pack_send(t)
        second(t, st, nr)

    for t in range(RO):
        pre_act(t)
    for t in range(RO):
        step(t, 0)
        step(t, 1)

    for c0, n, sem in ((0, 16, "dol"), (16, 8, "dol2")):
        ts(rr("endj", n, c0), rr("endi", n, c0), 4095, ALU.bitwise_and)
        cp(rr("endu", n, c0), rr("endj", n, c0))
        tt(rr("ylt", 16 * n, 16 * c0), IND(CH, rr("endu", n, c0)), rr("pres", 16 * n, 16 * c0), ALU.mult)
        dma("y", H(T.yl[:, 16 * c0:16 * (c0 + n)]), rr("ylt", 16 * n, 16 * c0), sem)
    dma("s", H(T.yx[:, WD - S:WD]), W2("lnd%d" % (RO - 1)), "dog", tok=arrived(RO - 1))

    if not ORDER:
        ORDER.extend(schedule(ops))
    count, clock, token = {}, {}, {}
    known = {e: {} for e in Q}

    def wait(e, tok):
        if known[e].get(tok[0], 0) >= tok[1]:
            return
        Q[e].wait_ge(T.sem[tok[0]], tok[1])
        known[e][tok[0]] = tok[1]
        for k, v in clock.get(tok, {}).items():
            known[e][k] = max(known[e].get(k, 0), v)

    for i in sorted(range(len(ops)), key=lambda k: (ORDER[k], k)):
        o = ops[i]
        need = {}
        for d, kind in o["deps"].items():
            if kind == 1:
                need[token[d][0]] = max(need.get(token[d][0], 0), token[d][1])
        if o["tok"]:
            need[o["tok"][0]] = o["tok"][1]
        for sem in sorted(need, key=lambda k: k == CNT.get(o["e"])):
            wait(o["e"], (sem, need[sem]))
        count[o["sem"]] = count.get(o["sem"], 0) + o["inc"]
        token[i] = (o["sem"], count[o["sem"]])
        clock[token[i]] = dict(known[o["e"]])
        call = o["fn"]()
        if call is not None:
            call.then_inc(T.sem[o["sem"]], o["inc"])
    for sem in sorted(count):
        wait("g", (sem, count[sem]))
